import numpy as np
import ml_dtypes


def mxq(x, axis, fmt="e4m3"):
    dtype, down = {"e4m3": (ml_dtypes.float8_e4m3fn, 7), "e5m2": (ml_dtypes.float8_e5m2, 14)}[fmt]
    v = np.moveaxis(np.asarray(x, np.float32).astype(ml_dtypes.bfloat16).astype(np.float64), axis, -1)
    blocks = v.reshape(v.shape[:-1] + (-1, 32))
    amax = np.abs(blocks).max(-1, keepdims=True)
    byte = np.maximum(np.where(amax > 0, np.frexp(amax)[1] - 1 + 127, 0) - down, 1)
    scale = np.exp2(byte - 127.0)
    codes = (blocks / scale).astype(np.float32).astype(dtype).astype(np.float64)
    return np.moveaxis((codes * scale).reshape(v.shape), -1, axis)


WIDE = False


def mx_kscale(k):
    if not WIDE:
        return np.ones(k)
    levels = np.array([10, -10, 5, -5, 0])
    if k % 512:
        return np.exp2(np.random.permutation(np.resize(levels, k // 32))).repeat(32)
    a = np.empty((k // 512, 16))
    for p in range(k // 512):
        a[p, :8] = np.random.permutation(np.resize(levels, 8))
        for g in range(8):
            far = levels[np.abs(levels - a[p, g]) >= 10]
            a[p, g + 8] = far[np.random.randint(len(far))]
    return np.exp2(a.ravel()).repeat(32)


def f64(x):
    return np.asarray(x).astype(np.float64)


def striped8(idx):
    return np.concatenate([x.reshape(-1, 16).T for x in idx]).astype(np.uint16)


def runs(offs, k):
    lists = np.stack([offs[16 * r : 16 * r + 16].T.reshape(-1) for r in range(8)]).astype(np.int64)
    return lists[np.arange(k) % 512 // 64]


def pack_weight(w):
    k, n = w.shape
    w = f64(np.asarray(w, np.float32).astype(ml_dtypes.bfloat16)).reshape(k // 32, 32, n)
    amax = np.abs(w).max(1)
    byte = np.clip(np.where(amax > 0, np.frexp(amax)[1] - 1 + 127 - 7, 1), 1, 254)
    scaled = (w * np.exp2(127.0 - byte)[:, None, :]).reshape(k, n).astype(np.float32)
    words = np.ascontiguousarray(scaled.reshape(k // 512, 128, 4, n).transpose(0, 1, 3, 2)).astype(ml_dtypes.float8_e4m3fn).view(np.uint8)
    return words, np.ascontiguousarray(byte.astype(np.uint8).reshape(k // 512, 16, n))


def unpack_weight(words, scales):
    g, p, n, _ = words.shape
    vals = np.ascontiguousarray(words).view(ml_dtypes.float8_e4m3fn).astype(np.float64) * np.repeat(np.exp2(scales.astype(np.float64) - 127.0), 8, axis=1)[..., None]
    return vals.transpose(0, 1, 3, 2).reshape(g * 512, n)


K, T, S, N, H = 512, 2048, 512, 512, 512


def setup_inputs():
    n = np.random.standard_normal
    s = mx_kscale(K)[:, None]
    u = mx_kscale(H)
    packed_xT = pack_weight(n((K, T)) * s)
    return {
        "x_words": packed_xT[0],
        "x_scales": packed_xT[1],
        "w1": (n((K, H)) / np.sqrt(K) / s).astype(np.float32),
        "gn": (np.random.uniform(0.5, 1.5, (H, 1)) * u[:, None]).astype(np.float32),
        "w2": (n((H, N)) / np.sqrt(H) / u[:, None]).astype(np.float32),
        "offs": striped8(np.random.randint(0, T, (8, S))),
        "n1": striped8(np.stack([np.random.permutation(S) for _ in range(8)])),
        "n2": striped8(np.stack([np.random.permutation(S) for _ in range(8)])),
        "n3": striped8(np.stack([np.random.permutation(S) for _ in range(8)])),
        "n4": striped8(np.stack([np.random.permutation(S) for _ in range(8)])),
    }


def reference(x_words, x_scales, w1, gn, w2, offs, n1, n2, n3, n4):
    xq = unpack_weight(x_words, x_scales)[np.arange(K)[:, None], runs(offs, K)]
    y = mxq(f64(w1), 0, "e4m3").T @ xq
    z = f64(gn) * ((y - (y[np.arange(H)[:, None], runs(n1, H)])) / (np.abs(y[np.arange(H)[:, None], runs(n2, H)] - y) + 0.5))
    h = mxq(f64(w2), 0, "e4m3").T @ mxq(z, 0, "e4m3")
    return 0.75 * (h[np.arange(N)[:, None], runs(n3, N)] + h[np.arange(N)[:, None], runs(n4, N)]) - h

from contextlib import ExitStack

import concourse.mybir as mybir

K, T, S, H, N = 512, 2048, 512, 512, 512
FLOPS = 2 * K * H * S + 2 * H * N * S

F32 = mybir.dt.float32
BF16 = mybir.dt.bfloat16
I32 = mybir.dt.int32
U32 = mybir.dt.uint32
U16 = mybir.dt.uint16
U8 = mybir.dt.uint8
FP8X4 = mybir.dt.float8_e4m3fn_x4
ALU = mybir.AluOpType
ACT = mybir.ActivationFunctionType

P = 128
PACK = 4
HALF = S // 2
GROUP = 16
TINY = 2.0 ** -100


def tile_picked_hashfraclap_none_p_kernel(tc, x_words, x_scales, w1, gn, w2, offs, n1, n2, n3, n4, out):
    nc = tc.nc
    with ExitStack() as ctx:
        keep = ctx.enter_context(tc.tile_pool(name="keep", bufs=1))
        psum = ctx.enter_context(tc.psum_pool(name="psum", bufs=1))

        def load_list(src, name):
            t = keep.tile([P, S // GROUP], U16, name=name)
            nc.sync.dma_start(t[:], src)
            return t

        def half_of(lst, h):
            return lst[:, h * HALF // GROUP : (h + 1) * HALF // GROUP]

        def cols(h):
            return slice(h * HALF, (h + 1) * HALF)

        def load_weight_half(w, h, name, tag):
            raw = keep.tile([P, PACK, HALF], F32, name=name, tag=tag)
            nc.sync.dma_start(raw[:], w.rearrange("(p j) c -> p j c", j=PACK)[:, :, cols(h)])
            return raw

        def deal_half(dealt, raw, h):
            dst = dealt[:].rearrange("p (t m j) -> p m j t", t=PACK, j=PACK)[:, h * 64 : (h + 1) * 64]
            nc.vector.tensor_copy(dst, raw[:].rearrange("p j (m t) -> p m j t", t=PACK))

        l_offs = load_list(offs, "l_offs")

        scale_win = keep.tile([P, T], U8, name="scale_win")
        scale_rows = x_scales[0].bitcast(I32)
        nc.scalar.dma_start(scale_win[:].bitcast(I32), scale_rows.unsqueeze(1).to_broadcast([16, 8, T // 4]))
        gain = keep.tile([P, PACK], F32, name="gain")
        nc.scalar.dma_start(gain[:], gn.rearrange("(p t) o -> p (t o)", t=PACK))

        word_win = keep.tile([P, T], I32, name="word_win", tag="first")
        nc.sync.dma_start(word_win[:], x_words[0].rearrange("p c r -> p (c r)").bitcast(I32))
        l_n2 = load_list(n2, "l_n2")
        w1_raw = [load_weight_half(w1, h, "w1_raw%d" % h, "w1_raw%d" % h) for h in range(2)]
        l_n1 = load_list(n1, "l_n1")


        picked_bytes = keep.tile([P, S], U8, name="picked_bytes")
        nc.vector.tensor_copy(picked_bytes[:], scale_win[:].indirect(l_offs[:]))
        x_plane = keep.tile([P, S], U8, name="x_plane", align_bytes=64)
        nc.vector.tensor_copy(x_plane[:].bitcast(I32), picked_bytes[:].bitcast(I32))
        for r in range(1, 4):
            queue = nc.sync if r == 2 else nc.scalar
            queue.dma_start(x_plane[r:P:32, :].bitcast(I32), picked_bytes[8 * r : P : 32, :].bitcast(I32))

        def small(name):
            return keep.tile([P, PACK], F32, name=name)

        pos, flip, neg, size, seed, e1, e2, fix, root = [small("g%d" % i) for i in range(9)]
        nc.vector.tensor_scalar(neg[:], gain[:], -1.0, TINY, ALU.mult, ALU.max)
        nc.vector.tensor_tensor(size[:], neg[:], gain[:], ALU.max)
        nc.scalar.activation(seed[:], size[:], ACT.Abs_reciprocal_sqrt)
        nc.vector.tensor_scalar(pos[:], gain[:], 0.0, None, ALU.is_gt)
        nc.vector.scalar_tensor_tensor(flip[:], gain[:], 0.0, pos[:], ALU.is_lt, ALU.subtract)
        nc.vector.tensor_tensor(e1[:], size[:], seed[:], ALU.mult)
        nc.vector.tensor_tensor(e2[:], e1[:], seed[:], ALU.mult)
        nc.vector.tensor_scalar(fix[:], e2[:], -0.5, 1.5, ALU.mult, ALU.add)
        nc.vector.tensor_tensor(root[:], e1[:], fix[:], ALU.mult)

        x_codes = keep.tile([P, S], U32, name="x_codes", align_bytes=64)
        nc.vector.tensor_copy(x_codes[:], word_win[:].bitcast(U32).indirect(l_offs[:]))

        l_n3 = load_list(n3, "l_n3")
        l_n4 = load_list(n4, "l_n4")

        w1_bf = keep.tile([P, PACK * H], BF16, name="w1_bf", align_bytes=64)
        w1_codes = keep.tile([P, H], U32, name="w1_codes", align_bytes=64)
        w1_plane = keep.tile([P, H], U8, name="w1_plane", align_bytes=64)
        for h in range(2):
            deal_half(w1_bf, w1_raw[h], h)
        w2_raw = [load_weight_half(w2, h, "w2_raw%d" % h, ("first", "w1_raw0")[h]) for h in range(2)]

        y_win, y_own = [], []
        for t in range(PACK):
            m = slice(t * P, (t + 1) * P)
            nc.vector.quantize_mx(w1_codes[:, m].bitcast(FP8X4), w1_plane[:, m], w1_bf[:, t * 512 : (t + 1) * 512])
            y_ps = psum.tile([P, S], F32, name="y_ps%d" % t)
            nc.tensor.matmul_mx(y_ps[:], w1_codes[:, m].bitcast(FP8X4), w1_plane[:, m], x_codes[:].bitcast(FP8X4), x_plane[:], start=True, stop=True)
            win = keep.tile([P, S], F32, name="y_win%d" % t)
            own = keep.tile([P, S], F32, name="y_own%d" % t)
            nc.scalar.activation(win[:], y_ps[:], ACT.Copy, scale=flip[:, t : t + 1])
            nc.scalar.activation(own[:], y_ps[:], ACT.Copy, scale=flip[:, t : t + 1])
            y_win.append(win)
            y_own.append(own)

        w2_bf = keep.tile([P, PACK * N], BF16, name="w2_bf", align_bytes=64)
        w2_codes = keep.tile([P, N], U32, name="w2_codes", align_bytes=64)
        w2_plane = keep.tile([P, N], U8, name="w2_plane", align_bytes=64)
        deal_half(w2_bf, w2_raw[0], 0)

        den = [keep.tile([P, PACK, HALF], F32, name="den%d" % h) for h in range(2)]
        num = [keep.tile([P, PACK, HALF], F32, name="num%d" % h) for h in range(2)]
        h_ps = [[psum.tile([P, 2, HALF], F32, name="h_ps%d_%d" % (h, u)) for u in range(2)] for h in range(2)]
        h_win = [keep.tile([P, S], F32, name="h_win%d" % t) for t in range(PACK)]
        h_own0 = keep.tile([P, S], F32, name="h_own0")

        def fetch_den(t, h):
            d = den[h][:, t, :]
            nc.vector.tensor_tensor(d, y_win[t][:].indirect(half_of(l_n2, h)), y_own[t][:, cols(h)], ALU.subtract)
            nc.scalar.activation(d, d, ACT.Abs)
            nc.scalar.activation(d, d, ACT.Abs_reciprocal_sqrt, bias=0.5)
            nc.scalar.activation(d, d, ACT.Square, scale=root[:, t : t + 1])

        def fetch_num(t, h):
            nc.vector.tensor_tensor(num[h][:, t, :], y_win[t][:].indirect(half_of(l_n1, h)), y_own[t][:, cols(h)], ALU.subtract)

        def second_product(h):
            z = keep.tile([P, HALF * PACK], BF16, name="z%d" % h, align_bytes=64)
            nc.vector.tensor_tensor(
                z[:].rearrange("p (c i t) -> p c t i", i=2, t=PACK),
                num[h][:].rearrange("p t (c i) -> p c t i", i=2),
                den[h][:].rearrange("p t (c i) -> p c t i", i=2),
                ALU.mult,
            )
            z_codes = keep.tile([P, HALF], U32, name="z_codes%d" % h, align_bytes=64)
            z_plane = keep.tile([P, HALF], U8, name="z_plane%d" % h, align_bytes=64)
            nc.vector.quantize_mx(z_codes[:].bitcast(FP8X4), z_plane[:], z[:])
            for t in range(PACK):
                m = slice(t * P, (t + 1) * P)
                acc = h_ps[h][t // 2][:, t % 2, :]
                nc.tensor.matmul_mx(acc, w2_codes[:, m].bitcast(FP8X4), w2_plane[:, m], z_codes[:].bitcast(FP8X4), z_plane[:], start=True, stop=True)
            for t in range(PACK):
                acc = h_ps[h][t // 2][:, t % 2, :]
                nc.scalar.activation(h_win[t][:, cols(h)], acc, ACT.Copy, scale=0.75)
                if t == 0:
                    nc.scalar.copy(h_own0[:, cols(h)], acc)

        for t in range(PACK):
            fetch_den(t, 0)
            fetch_num(t, 0)
        deal_half(w2_bf, w2_raw[1], 1)
        nc.vector.quantize_mx(w2_codes[:].bitcast(FP8X4), w2_plane[:], w2_bf[:])
        for t in range(PACK):
            fetch_den(t, 1)
        second_product(0)
        for t in range(PACK):
            fetch_num(t, 1)
        second_product(1)

        out_rows = out.rearrange("(p t) s -> p t s", t=PACK)
        for t in range(PACK):
            for h in range(2):
                acc = h_ps[h][t // 2][:, t % 2, :]
                part = keep.tile([P, HALF], F32, name="part%d_%d" % (t, h))
                res = keep.tile([P, HALF], F32, name="res%d_%d" % (t, h))
                if t == 0:
                    nc.vector.tensor_tensor(part[:], h_win[t][:].indirect(half_of(l_n3, h)), h_own0[:, cols(h)], ALU.subtract)
                else:
                    got = keep.tile([P, HALF], F32, name="got%d_%d" % (t, h))
                    nc.scalar.activation(got[:], h_win[t][:].indirect(half_of(l_n3, h)), ACT.Copy)
                    nc.vector.tensor_tensor(part[:], got[:], acc, ALU.subtract)
                if t == 3:
                    got4 = keep.tile([P, HALF], F32, name="got4_%d" % h)
                    nc.scalar.activation(got4[:], h_win[t][:].indirect(half_of(l_n4, h)), ACT.Copy)
                    nc.vector.tensor_tensor(res[:], got4[:], part[:], ALU.add)
                else:
                    nc.vector.tensor_tensor(res[:], h_win[t][:].indirect(half_of(l_n4, h)), part[:], ALU.add)
                nc.sync.dma_start(out_rows[:, t, cols(h)], res[:])
